import numpy as np
import ml_dtypes


def mxq(x, axis, fmt="e4m3"):
    dtype, down = {"e4m3": (ml_dtypes.float8_e4m3fn, 7), "e5m2": (ml_dtypes.float8_e5m2, 14)}[fmt]
    v = np.moveaxis(np.asarray(x, np.float32).astype(ml_dtypes.bfloat16).astype(np.float64), axis, -1)
    blocks = v.reshape(v.shape[:-1] + (-1, 32))
    amax = np.abs(blocks).max(-1, keepdims=True)
    byte = np.maximum(np.where(amax > 0, np.frexp(amax)[1] - 1 + 127, 0) - down, 1)
    scale = np.exp2(byte - 127.0)
    codes = (blocks / scale).astype(np.float32).astype(dtype).astype(np.float64)
    return np.moveaxis((codes * scale).reshape(v.shape), -1, axis)


WIDE = False


def mx_kscale(k):
    if not WIDE:
        return np.ones(k)
    levels = np.array([30, -30])
    if k % 512:
        return np.exp2(np.random.permutation(np.resize(levels, k // 32))).repeat(32)
    a = np.empty((k // 512, 16))
    for p in range(k // 512):
        a[p, :8] = np.random.permutation(np.resize(levels, 8))
        for g in range(8):
            far = levels[np.abs(levels - a[p, g]) >= 10]
            a[p, g + 8] = far[np.random.randint(len(far))]
    return np.exp2(a.ravel()).repeat(32)


def f64(x):
    return np.asarray(x).astype(np.float64)


def striped(idx):
    return np.tile(np.asarray(idx).reshape(-1, 16).T, (8, 1)).astype(np.uint16)


def unstriped(offs):
    return offs[:16].T.reshape(-1).astype(np.int64)


E2M1 = np.array([0.0, 0.5, 1.0, 1.5, 2.0, 3.0, 4.0, 6.0, -0.0, -0.5, -1.0, -1.5, -2.0, -3.0, -4.0, -6.0])


def pack_weight(w, fmt):
    k, n = w.shape
    w = f64(np.asarray(w, np.float32).astype(ml_dtypes.bfloat16)).reshape(k // 32, 32, n)
    amax = np.abs(w).max(1)
    if fmt == "e4m3":
        byte = np.frexp(amax)[1] - 1 + 127 - 7
    else:
        mant, ex = np.frexp(amax / 6.0)
        byte = np.where(mant > 0.5, ex, ex - 1) + 127
    byte = np.clip(np.where(amax > 0, byte, 1), 1, 254)
    scaled = (w * np.exp2(127.0 - byte)[:, None, :]).reshape(k, n).astype(np.float32)
    by_word = np.ascontiguousarray(scaled.reshape(k // 512, 128, 4, n).transpose(0, 1, 3, 2))
    if fmt == "e4m3":
        words = by_word.astype(ml_dtypes.float8_e4m3fn).view(np.uint8)
    else:
        c = by_word.astype(ml_dtypes.float4_e2m1fn).view(np.uint8) & 0xF
        words = (c[..., 0::2] | (c[..., 1::2] << 4)).reshape(k // 512, 128, 2 * n)
    return np.ascontiguousarray(words), np.ascontiguousarray(byte.astype(np.uint8).reshape(k // 512, 16, n))


def unpack_weight(words, scales, fmt):
    g, _, n = scales.shape
    words = np.ascontiguousarray(words).reshape(g, 128, n, -1)
    if fmt == "e4m3":
        vals = words.view(ml_dtypes.float8_e4m3fn).astype(np.float64)
    else:
        nib = np.empty((g, 128, n, 4), np.uint8)
        nib[..., 0::2] = words & 0xF
        nib[..., 1::2] = words >> 4
        vals = E2M1[nib]
    vals = vals * np.repeat(np.exp2(scales.astype(np.float64) - 127.0), 8, axis=1)[..., None]
    return vals.transpose(0, 1, 3, 2).reshape(g * 512, n)


K, T, J, S, R, L, N, C = 1024, 1024, 256, 512, 512, 512, 256, 1024


def setup_inputs():
    n = np.random.standard_normal
    idx = np.random.permutation(T)[:J]
    idx2 = np.random.permutation(S)[:J]
    idx3 = np.random.permutation(C)[:J]
    fk = mx_kscale(K)
    fr = mx_kscale(R)
    fl = mx_kscale(L)
    wp = pack_weight(n((K, R)) * 1 / np.sqrt(K) * fk[:, None] * fr, "e2m1")
    sxp = pack_weight(n((L, J)) / fl[:, None], "e2m1")
    wsp = pack_weight(n((L, R)) * 1 / np.sqrt(L) * fl[:, None] * fr, "e2m1")
    wbp = pack_weight(n((R, N)) * 1 / np.sqrt(R) / fr[:, None], "e4m3")
    return {
        "xa": (n((K, T))).astype(np.float32),
        "xb": (n((K, S))).astype(np.float32),
        "fk": (np.random.uniform(0.5, 2.0, (K, 1)) / fk[:, None]).astype(np.float32),
        "w_words": wp[0],
        "w_scales": wp[1],
        "sx_words": sxp[0],
        "sx_scales": sxp[1],
        "ws_words": wsp[0],
        "ws_scales": wsp[1],
        "wb_words": wbp[0],
        "wb_scales": wbp[1],
        "old": (1.0 * n((N, C))).astype(np.float32),
        "offs": striped(idx),
        "offs2": striped(idx2),
        "offs3": striped(idx3),
    }


def reference(xa, xb, fk, w_words, w_scales, sx_words, sx_scales, ws_words, ws_scales, wb_words, wb_scales, old, offs, offs2, offs3):
    idx = unstriped(offs)
    idx2 = unstriped(offs2)
    idx3 = unstriped(offs3)
    wu = unpack_weight(w_words, w_scales, "e2m1")
    sxu = unpack_weight(sx_words, sx_scales, "e2m1")
    wsu = unpack_weight(ws_words, ws_scales, "e2m1")
    wbu = unpack_weight(wb_words, wb_scales, "e4m3")
    u = f64(xa)[:, idx] * f64(xb)[:, idx2] * f64(fk)
    uq = mxq(u, 0, "e4m3")
    a = wu.T @ uq
    b2 = wsu.T @ sxu
    hid = np.maximum(a, b2)
    hidq = mxq(hid, 0, "e5m2")
    p = wbu.T @ hidq
    pp = np.zeros((N, C))
    pp[:, idx3] = p
    y = pp + 0.5 * f64(old)
    return y

@@ -1,0 +1,229 @@
+from contextlib import ExitStack
+
+import concourse.mybir as mybir
+
+K, T, J, S, R, L, N, C = 1024, 1024, 256, 512, 512, 512, 256, 1024
+FLOPS = 2 * (K * R * J + L * R * J + R * N * J)
+
+F32 = mybir.dt.float32
+BF16 = mybir.dt.bfloat16
+I32 = mybir.dt.int32
+U32 = mybir.dt.uint32
+U16 = mybir.dt.uint16
+U8 = mybir.dt.uint8
+E4M3 = mybir.dt.float8_e4m3fn_x4
+E5M2 = mybir.dt.float8_e5m2_x4
+E2M1 = mybir.dt.float4_e2m1fn_x4
+ALU = mybir.AluOpType
+COPY = mybir.ActivationFunctionType.Copy
+
+P = 128
+PACK = 4
+K_PASS = P * PACK
+PASSES = K // K_PASS
+HALF = 128
+HALVES = J // HALF
+N_TILES = N // P
+STORE_COLS = 512
+
+
+def load_scale_rows(queue, plane, rows):
+    for q in range(4):
+        queue.dma_start(
+            out=plane[32 * q : 32 * q + 4].bitcast(I32),
+            in_=rows[:, 4 * q : 4 * q + 4, :].rearrange("z r c -> r z c").bitcast(I32),
+        )
+
+
+def interleave(copy, dst, src):
+    copy(
+        dst.rearrange("p (c i) t -> p c t i", i=4),
+        src.rearrange("p t (c i) -> p c t i", i=4),
+    )
+
+
+def tile_list_entryproducts_rival_scattered_kernel(
+    tc, xa, xb, fk, w_words, w_scales, sx_words, sx_scales, ws_words, ws_scales, wb_words, wb_scales, old, offs, offs2, offs3, out
+):
+    nc = tc.nc
+    with ExitStack() as ctx:
+        sb = ctx.enter_context(tc.tile_pool(name="sb", bufs=1))
+        ps = ctx.enter_context(tc.psum_pool(name="ps", bufs=1))
+
+        list_a = sb.tile([P, J // 16], U16, name="list_a")
+        list_b = sb.tile([P, J // 16], U16, name="list_b")
+        list_out = sb.tile([P, J // 16], U16, name="list_out")
+        fk_sb = sb.tile([P, PASSES, PACK], F32, name="fk_sb")
+        xa_sb = [[sb.tile([P, T], F32, name=f"xa_{z}_{t}") for t in range(PACK)] for z in range(PASSES)]
+        xb_sb = [sb.tile([P, PACK, S], F32, name=f"xb_{z}") for z in range(PASSES)]
+        old_sb = sb.tile([P, N_TILES, C], F32, name="old_sb")
+
+        w_raw = sb.tile([P, PASSES, 2 * R], U8, name="w_raw", align_bytes=64)
+        ws_raw = sb.tile([P, 1, 2 * R], U8, name="ws_raw", align_bytes=64)
+        w_dealt = sb.tile([P, PASSES, 2 * R], U8, name="w_dealt", align_bytes=64)
+        ws_dealt = sb.tile([P, 1, 2 * R], U8, name="ws_dealt", align_bytes=64)
+        w_sc_raw = sb.tile([P, PASSES, R], U8, name="w_sc_raw", align_bytes=64)
+        ws_sc_raw = sb.tile([P, 1, R], U8, name="ws_sc_raw", align_bytes=64)
+        w_sc = sb.tile([P, PASSES, R], U8, name="w_sc", align_bytes=64)
+        ws_sc = sb.tile([P, 1, R], U8, name="ws_sc", align_bytes=64)
+        sx_sb = sb.tile([P, 2 * J], U8, name="sx_sb", align_bytes=64)
+        sx_sc = sb.tile([P, 1, J], U8, name="sx_sc", align_bytes=64)
+        wb_sb = sb.tile([P, N], U32, name="wb_sb", align_bytes=64)
+        wb_sc = sb.tile([P, 1, N], U8, name="wb_sc", align_bytes=64)
+        pages = [sb.tile([P, C], F32, name=f"page_{nt}") for nt in range(N_TILES)]
+
+        def load_xa(z, t):
+            rows = xa[K_PASS * z : K_PASS * (z + 1), :].rearrange("(p t) c -> p t c", t=PACK)
+            nc.sync.dma_start(out=xa_sb[z][t][:], in_=rows[:, t, :])
+
+        def load_xb(z):
+            rows = xb[K_PASS * z : K_PASS * (z + 1), :].rearrange("(p t) c -> p t c", t=PACK)
+            nc.sync.dma_start(out=xb_sb[z][:], in_=rows)
+
+        nc.vector.memset(w_sc_raw[:].bitcast(I32), 0)
+        nc.vector.memset(sx_sc[:].bitcast(I32), 0)
+        nc.vector.memset(wb_sc[:].bitcast(I32), 0)
+        for nt in range(N_TILES):
+            nc.vector.memset(pages[nt][:], 0.0)
+        nc.gpsimd.memset(ws_sc_raw[:].bitcast(I32), 0)
+        nc.gpsimd.dma_start(out=fk_sb[:], in_=fk.rearrange("(z p t) o -> p z (t o)", p=P, t=PACK))
+        load_scale_rows(nc.gpsimd, ws_sc_raw, ws_scales)
+
+        load_xb(0)
+        nc.sync.dma_start(list_b[:], offs2)
+        load_xa(0, 0)
+        nc.sync.dma_start(list_a[:], offs)
+        load_xa(0, 1)
+        nc.sync.dma_start(out=w_raw[:].bitcast(I32), in_=w_words.rearrange("z p c -> p z c").bitcast(I32))
+        load_xb(1)
+        load_scale_rows(nc.sync, w_sc_raw, w_scales)
+        load_xa(0, 2)
+        load_xa(0, 3)
+        nc.sync.dma_start(out=ws_raw[:].bitcast(I32), in_=ws_words.rearrange("z p c -> p z c").bitcast(I32))
+        nc.sync.dma_start(out=sx_sb[:].bitcast(I32), in_=sx_words[0].bitcast(I32))
+        load_xa(1, 0)
+        load_xa(1, 1)
+        load_scale_rows(nc.sync, sx_sc, sx_scales)
+        load_xa(1, 2)
+        load_xa(1, 3)
+        nc.sync.dma_start(out=wb_sb[:].bitcast(I32), in_=wb_words[0].rearrange("p n t -> p (n t)").bitcast(I32))
+        load_scale_rows(nc.sync, wb_sc, wb_scales)
+        nc.sync.dma_start(list_out[:], offs3)
+        nc.sync.dma_start(out=old_sb[:], in_=old.rearrange("(nt p) c -> p nt c", p=P))
+
+        def deal(dst, src):
+            nc.vector.tensor_copy(
+                dst.rearrange("p z (t m) -> p z t m", t=PACK), src.rearrange("p z (m t) -> p z t m", t=PACK)
+            )
+
+        deal(w_dealt[:].bitcast(U16), w_raw[:].bitcast(U16))
+        deal(ws_dealt[:].bitcast(U16), ws_raw[:].bitcast(U16))
+        deal(w_sc[:], w_sc_raw[:])
+        deal(ws_sc[:], ws_sc_raw[:])
+
+        def stationary(dealt, scales, z, t):
+            return dict(
+                lhsT=dealt[:, z, 2 * P * t : 2 * P * (t + 1)].bitcast(E2M1),
+                lhsT_scale=scales[:, z, P * t : P * (t + 1)],
+            )
+
+        picked_b = [sb.tile([P, PACK, J], F32, name=f"picked_b_{z}") for z in range(PASSES)]
+        factor = [sb.tile([P, PACK, J], F32, name=f"factor_{z}") for z in range(PASSES)]
+        for z in range(PASSES):
+            for t in range(PACK):
+                nc.scalar.activation(picked_b[z][:, t, :], xb_sb[z][:, t, :].indirect(list_b[:]), COPY)
+                nc.scalar.activation(factor[z][:, t, :], picked_b[z][:, t, :], COPY, scale=fk_sb[:, z, t : t + 1])
+
+        rival = [sb.tile([P, HALF, PACK], F32, name=f"rival_{h}") for h in range(HALVES)]
+        for h in range(HALVES):
+            rival_ps = ps.tile([P, PACK, HALF], F32, name=f"rival_ps_{h}")
+            for t in range(PACK):
+                nc.tensor.matmul_mx(
+                    out=rival_ps[:, t, :],
+                    rhs=sx_sb[:, 2 * HALF * h : 2 * HALF * (h + 1)].bitcast(E2M1),
+                    rhs_scale=sx_sc[:, 0, HALF * h : HALF * (h + 1)],
+                    start=True,
+                    stop=True,
+                    **stationary(ws_dealt, ws_sc, 0, t),
+                )
+            nc.scalar.copy(rival[h][:], rival_ps[:].rearrange("p t j -> p j t"))
+
+        u = [sb.tile([P, PACK, J], F32, name=f"u_{z}") for z in range(PASSES)]
+        first_ps = [ps.tile([P, PACK, HALF], F32, name=f"first_ps_{h}") for h in range(HALVES)]
+
+        def first_product(z, h, codes, scales):
+            for t in range(PACK):
+                nc.tensor.matmul_mx(
+                    out=first_ps[h][:, t, :],
+                    rhs=codes.bitcast(E4M3),
+                    rhs_scale=scales,
+                    start=(z == 0 and t == 0),
+                    stop=(z == PASSES - 1 and t == PACK - 1),
+                    **stationary(w_dealt, w_sc, z, t),
+                )
+
+        for t in range(PACK):
+            nc.vector.tensor_tensor(u[0][:, t, :], xa_sb[0][t][:].indirect(list_a[:]), factor[0][:, t, :], ALU.mult)
+        u0_bf = sb.tile([P, J, PACK], BF16, name="u0_bf", align_bytes=64)
+        u0_codes = sb.tile([P, J], U32, name="u0_codes", align_bytes=64)
+        u0_sc = sb.tile([P, J], U8, name="u0_sc", align_bytes=64)
+        interleave(nc.scalar.copy, u0_bf[:], u[0][:])
+        nc.vector.quantize_mx(out=u0_codes[:].bitcast(E4M3), scales=u0_sc[:], in_=u0_bf[:].rearrange("p j t -> p (j t)"))
+        for h in range(HALVES):
+            cols = slice(HALF * h, HALF * (h + 1))
+            first_product(0, h, u0_codes[:, cols], u0_sc[:, cols])
+
+        for t in range(PACK - 1):
+            nc.vector.tensor_tensor(u[1][:, t, :], xa_sb[1][t][:].indirect(list_a[:]), factor[1][:, t, :], ALU.mult)
+        t = PACK - 1
+        for h in range(HALVES):
+            cols = slice(HALF * h, HALF * (h + 1))
+            nc.vector.tensor_tensor(
+                u[1][:, t, cols], xa_sb[1][t][:].indirect(list_a[:, 8 * h : 8 * (h + 1)]), factor[1][:, t, cols], ALU.mult
+            )
+        u1_bf = [sb.tile([P, HALF, PACK], BF16, name=f"u1_bf_{h}", align_bytes=64) for h in range(HALVES)]
+        u1_codes = [sb.tile([P, HALF], U32, name=f"u1_codes_{h}", align_bytes=64) for h in range(HALVES)]
+        u1_sc = [sb.tile([P, HALF], U8, name=f"u1_sc_{h}", align_bytes=64) for h in range(HALVES)]
+        weavers = [nc.scalar.copy, nc.vector.tensor_copy]
+        for h in range(HALVES):
+            interleave(weavers[h], u1_bf[h][:], u[1][:, :, HALF * h : HALF * (h + 1)])
+        for h in range(HALVES):
+            nc.vector.quantize_mx(
+                out=u1_codes[h][:].bitcast(E4M3), scales=u1_sc[h][:], in_=u1_bf[h][:].rearrange("p j t -> p (j t)")
+            )
+            first_product(1, h, u1_codes[h][:], u1_sc[h][:])
+
+        result = [[sb.tile([P, HALF], F32, name=f"result_{nt}_{h}") for h in range(HALVES)] for nt in range(N_TILES)]
+        for h in range(HALVES):
+            hid_bf = sb.tile([P, HALF, PACK], BF16, name=f"hid_bf_{h}", align_bytes=64)
+            hid_codes = sb.tile([P, HALF], U32, name=f"hid_codes_{h}", align_bytes=64)
+            hid_sc = sb.tile([P, HALF], U8, name=f"hid_sc_{h}", align_bytes=64)
+            nc.vector.tensor_tensor(hid_bf[:], first_ps[h][:].rearrange("p t j -> p j t"), rival[h][:], ALU.max)
+            nc.vector.quantize_mx(out=hid_codes[:].bitcast(E5M2), scales=hid_sc[:], in_=hid_bf[:].rearrange("p j t -> p (j t)"))
+            for nt in range(N_TILES):
+                second_ps = ps.tile([P, HALF], F32, name=f"second_ps_{nt}_{h}")
+                nc.tensor.matmul_mx(
+                    out=second_ps[:],
+                    lhsT=wb_sb[:, P * nt : P * (nt + 1)].bitcast(E4M3),
+                    lhsT_scale=wb_sc[:, 0, P * nt : P * (nt + 1)],
+                    rhs=hid_codes[:].bitcast(E5M2),
+                    rhs_scale=hid_sc[:],
+                    start=True,
+                    stop=True,
+                )
+                if nt == 0 and h == 1:
+                    nc.vector.tensor_copy(result[nt][h][:], second_ps[:])
+                else:
+                    nc.scalar.copy(result[nt][h][:], second_ps[:])
+
+        for h in range(HALVES):
+            places = list_out[:, 8 * h : 8 * (h + 1)]
+            nc.vector.tensor_copy(pages[0][:].indirect(places), result[0][h][:])
+            nc.scalar.activation(pages[1][:].indirect(places), result[1][h][:], COPY)
+
+        for nt in range(N_TILES):
+            for c0 in range(0, C, STORE_COLS):
+                cols = slice(c0, c0 + STORE_COLS)
+                y = sb.tile([P, STORE_COLS], F32, name=f"y_{nt}_{c0}")
+                nc.vector.scalar_tensor_tensor(y[:], old_sb[:, nt, cols], 0.5, pages[nt][:, cols], ALU.mult, ALU.add)
+                nc.sync.dma_start(out=out[P * nt : P * (nt + 1), cols], in_=y[:])

@@ -24,7 +24,7 @@ PASSES = K // K_PASS
 HALF = 128
 HALVES = J // HALF
 N_TILES = N // P
-STORE_COLS = 512
+STORE_WIDTHS = ((256, 256, 512), (512, 256, 256))
 
 
 def load_scale_rows(queue, plane, rows):
@@ -80,33 +80,47 @@ def tile_list_entryproducts_rival_scattered_kernel(
             rows = xb[K_PASS * z : K_PASS * (z + 1), :].rearrange("(p t) c -> p t c", t=PACK)
             nc.sync.dma_start(out=xb_sb[z][:], in_=rows)
 
+        def load_words(dst, src):
+            nc.sync.dma_start(out=dst.bitcast(I32), in_=src.bitcast(I32))
+
+        def load_scale_quadrant(plane, rows, q):
+            nc.sync.dma_start(
+                out=plane[32 * q : 32 * q + 4].bitcast(I32),
+                in_=rows[:, 4 * q : 4 * q + 4, :].rearrange("z r c -> r z c").bitcast(I32),
+            )
+
         nc.vector.memset(w_sc_raw[:].bitcast(I32), 0)
+        nc.vector.memset(ws_sc_raw[:].bitcast(I32), 0)
         nc.vector.memset(sx_sc[:].bitcast(I32), 0)
         nc.vector.memset(wb_sc[:].bitcast(I32), 0)
         for nt in range(N_TILES):
             nc.vector.memset(pages[nt][:], 0.0)
-        nc.gpsimd.memset(ws_sc_raw[:].bitcast(I32), 0)
-        nc.gpsimd.dma_start(out=fk_sb[:], in_=fk.rearrange("(z p t) o -> p z (t o)", p=P, t=PACK))
-        load_scale_rows(nc.gpsimd, ws_sc_raw, ws_scales)
 
         load_xb(0)
         nc.sync.dma_start(list_b[:], offs2)
+        nc.sync.dma_start(out=fk_sb[:], in_=fk.rearrange("(z p t) o -> p z (t o)", p=P, t=PACK))
         load_xa(0, 0)
         nc.sync.dma_start(list_a[:], offs)
+        load_words(w_raw[:], w_words.rearrange("z p c -> p z c"))
         load_xa(0, 1)
-        nc.sync.dma_start(out=w_raw[:].bitcast(I32), in_=w_words.rearrange("z p c -> p z c").bitcast(I32))
+        for q in range(3):
+            load_scale_quadrant(w_sc_raw, w_scales, q)
         load_xb(1)
-        load_scale_rows(nc.sync, w_sc_raw, w_scales)
+        load_scale_quadrant(w_sc_raw, w_scales, 3)
+        load_words(ws_raw[:], ws_words.rearrange("z p c -> p z c"))
+        load_scale_quadrant(ws_sc_raw, ws_scales, 0)
         load_xa(0, 2)
+        for q in range(1, 4):
+            load_scale_quadrant(ws_sc_raw, ws_scales, q)
         load_xa(0, 3)
-        nc.sync.dma_start(out=ws_raw[:].bitcast(I32), in_=ws_words.rearrange("z p c -> p z c").bitcast(I32))
-        nc.sync.dma_start(out=sx_sb[:].bitcast(I32), in_=sx_words[0].bitcast(I32))
+        load_words(sx_sb[:], sx_words[0])
+        load_scale_quadrant(sx_sc, sx_scales, 0)
         load_xa(1, 0)
-        load_xa(1, 1)
-        load_scale_rows(nc.sync, sx_sc, sx_scales)
-        load_xa(1, 2)
-        load_xa(1, 3)
-        nc.sync.dma_start(out=wb_sb[:].bitcast(I32), in_=wb_words[0].rearrange("p n t -> p (n t)").bitcast(I32))
+        for q in range(1, 4):
+            load_scale_quadrant(sx_sc, sx_scales, q)
+        for t in range(1, PACK):
+            load_xa(1, t)
+        load_words(wb_sb[:], wb_words[0].rearrange("p n t -> p (n t)"))
         load_scale_rows(nc.sync, wb_sc, wb_scales)
         nc.sync.dma_start(list_out[:], offs3)
         nc.sync.dma_start(out=old_sb[:], in_=old.rearrange("(nt p) c -> p nt c", p=P))
@@ -116,11 +130,6 @@ def tile_list_entryproducts_rival_scattered_kernel(
                 dst.rearrange("p z (t m) -> p z t m", t=PACK), src.rearrange("p z (m t) -> p z t m", t=PACK)
             )
 
-        deal(w_dealt[:].bitcast(U16), w_raw[:].bitcast(U16))
-        deal(ws_dealt[:].bitcast(U16), ws_raw[:].bitcast(U16))
-        deal(w_sc[:], w_sc_raw[:])
-        deal(ws_sc[:], ws_sc_raw[:])
-
         def stationary(dealt, scales, z, t):
             return dict(
                 lhsT=dealt[:, z, 2 * P * t : 2 * P * (t + 1)].bitcast(E2M1),
@@ -129,27 +138,18 @@ def tile_list_entryproducts_rival_scattered_kernel(
 
         picked_b = [sb.tile([P, PACK, J], F32, name=f"picked_b_{z}") for z in range(PASSES)]
         factor = [sb.tile([P, PACK, J], F32, name=f"factor_{z}") for z in range(PASSES)]
-        for z in range(PASSES):
+        u = [sb.tile([P, PACK, J], F32, name=f"u_{z}") for z in range(PASSES)]
+        rival = [sb.tile([P, HALF, PACK], F32, name=f"rival_{h}") for h in range(HALVES)]
+
+        def pick_b(z):
             for t in range(PACK):
                 nc.scalar.activation(picked_b[z][:, t, :], xb_sb[z][:, t, :].indirect(list_b[:]), COPY)
                 nc.scalar.activation(factor[z][:, t, :], picked_b[z][:, t, :], COPY, scale=fk_sb[:, z, t : t + 1])
 
-        rival = [sb.tile([P, HALF, PACK], F32, name=f"rival_{h}") for h in range(HALVES)]
-        for h in range(HALVES):
-            rival_ps = ps.tile([P, PACK, HALF], F32, name=f"rival_ps_{h}")
-            for t in range(PACK):
-                nc.tensor.matmul_mx(
-                    out=rival_ps[:, t, :],
-                    rhs=sx_sb[:, 2 * HALF * h : 2 * HALF * (h + 1)].bitcast(E2M1),
-                    rhs_scale=sx_sc[:, 0, HALF * h : HALF * (h + 1)],
-                    start=True,
-                    stop=True,
-                    **stationary(ws_dealt, ws_sc, 0, t),
-                )
-            nc.scalar.copy(rival[h][:], rival_ps[:].rearrange("p t j -> p j t"))
-
-        u = [sb.tile([P, PACK, J], F32, name=f"u_{z}") for z in range(PASSES)]
-        first_ps = [ps.tile([P, PACK, HALF], F32, name=f"first_ps_{h}") for h in range(HALVES)]
+        def pick_a(z, t, first, count):
+            cols = slice(first, first + count)
+            entries = list_a[:, first // 16 : (first + count) // 16]
+            nc.vector.tensor_tensor(u[z][:, t, cols], xa_sb[z][t][:].indirect(entries), factor[z][:, t, cols], ALU.mult)
 
         def first_product(z, h, codes, scales):
             for t in range(PACK):
@@ -162,29 +162,49 @@ def tile_list_entryproducts_rival_scattered_kernel(
                     **stationary(w_dealt, w_sc, z, t),
                 )
 
-        for t in range(PACK):
-            nc.vector.tensor_tensor(u[0][:, t, :], xa_sb[0][t][:].indirect(list_a[:]), factor[0][:, t, :], ALU.mult)
+        pick_b(0)
+        pick_a(0, 0, 0, J)
+        deal(w_dealt[:].bitcast(U16), w_raw[:].bitcast(U16))
+        pick_a(0, 1, 0, J)
+        pick_b(1)
+        deal(w_sc[:], w_sc_raw[:])
+        deal(ws_dealt[:].bitcast(U16), ws_raw[:].bitcast(U16))
+        pick_a(0, 2, 0, J)
+        pick_a(0, 3, 0, J)
         u0_bf = sb.tile([P, J, PACK], BF16, name="u0_bf", align_bytes=64)
         u0_codes = sb.tile([P, J], U32, name="u0_codes", align_bytes=64)
         u0_sc = sb.tile([P, J], U8, name="u0_sc", align_bytes=64)
         interleave(nc.scalar.copy, u0_bf[:], u[0][:])
+        deal(ws_sc[:], ws_sc_raw[:])
+        pick_a(1, 0, 0, J)
+        pick_a(1, 1, 0, J)
+        for h in range(HALVES):
+            rival_ps = ps.tile([P, PACK, HALF], F32, name=f"rival_ps_{h}", tag=f"hidden_{h}")
+            for t in range(PACK):
+                nc.tensor.matmul_mx(
+                    out=rival_ps[:, t, :],
+                    rhs=sx_sb[:, 2 * HALF * h : 2 * HALF * (h + 1)].bitcast(E2M1),
+                    rhs_scale=sx_sc[:, 0, HALF * h : HALF * (h + 1)],
+                    start=True,
+                    stop=True,
+                    **stationary(ws_dealt, ws_sc, 0, t),
+                )
+            nc.scalar.copy(rival[h][:], rival_ps[:].rearrange("p t j -> p j t"))
+
+        first_ps = [ps.tile([P, PACK, HALF], F32, name=f"first_ps_{h}", tag=f"hidden_{h}") for h in range(HALVES)]
         nc.vector.quantize_mx(out=u0_codes[:].bitcast(E4M3), scales=u0_sc[:], in_=u0_bf[:].rearrange("p j t -> p (j t)"))
         for h in range(HALVES):
             cols = slice(HALF * h, HALF * (h + 1))
             first_product(0, h, u0_codes[:, cols], u0_sc[:, cols])
-
-        for t in range(PACK - 1):
-            nc.vector.tensor_tensor(u[1][:, t, :], xa_sb[1][t][:].indirect(list_a[:]), factor[1][:, t, :], ALU.mult)
-        t = PACK - 1
-        for h in range(HALVES):
-            cols = slice(HALF * h, HALF * (h + 1))
-            nc.vector.tensor_tensor(
-                u[1][:, t, cols], xa_sb[1][t][:].indirect(list_a[:, 8 * h : 8 * (h + 1)]), factor[1][:, t, cols], ALU.mult
-            )
+        pick_a(1, 2, 0, J)
+        pick_a(1, 3, 0, HALF)
+        picked_a = sb.tile([P, HALF], F32, name="picked_a")
+        nc.scalar.activation(picked_a[:], xa_sb[1][3][:].indirect(list_a[:, HALF // 16 :]), COPY)
+        nc.vector.tensor_tensor(u[1][:, 3, HALF:], picked_a[:], factor[1][:, 3, HALF:], ALU.mult)
         u1_bf = [sb.tile([P, HALF, PACK], BF16, name=f"u1_bf_{h}", align_bytes=64) for h in range(HALVES)]
         u1_codes = [sb.tile([P, HALF], U32, name=f"u1_codes_{h}", align_bytes=64) for h in range(HALVES)]
         u1_sc = [sb.tile([P, HALF], U8, name=f"u1_sc_{h}", align_bytes=64) for h in range(HALVES)]
-        weavers = [nc.scalar.copy, nc.vector.tensor_copy]
+        weavers = [nc.vector.tensor_copy, nc.vector.tensor_copy]
         for h in range(HALVES):
             interleave(weavers[h], u1_bf[h][:], u[1][:, :, HALF * h : HALF * (h + 1)])
         for h in range(HALVES):
@@ -193,7 +213,11 @@ def tile_list_entryproducts_rival_scattered_kernel(
             )
             first_product(1, h, u1_codes[h][:], u1_sc[h][:])
 
-        result = [[sb.tile([P, HALF], F32, name=f"result_{nt}_{h}") for h in range(HALVES)] for nt in range(N_TILES)]
+        lead_ps = ps.tile([P, HALF], F32, name="lead_ps")
+        rest_ps = ps.tile([P, 3, HALF], F32, name="rest_ps")
+        second_ps = {(0, 0): lead_ps[:], (0, 1): rest_ps[:, 0, :], (1, 0): rest_ps[:, 1, :], (1, 1): rest_ps[:, 2, :]}
+        lead = sb.tile([P, HALF], F32, name="lead")
+        rest = sb.tile([P, 3 * HALF], F32, name="rest")
         for h in range(HALVES):
             hid_bf = sb.tile([P, HALF, PACK], BF16, name=f"hid_bf_{h}", align_bytes=64)
             hid_codes = sb.tile([P, HALF], U32, name=f"hid_codes_{h}", align_bytes=64)
@@ -201,9 +225,8 @@ def tile_list_entryproducts_rival_scattered_kernel(
             nc.vector.tensor_tensor(hid_bf[:], first_ps[h][:].rearrange("p t j -> p j t"), rival[h][:], ALU.max)
             nc.vector.quantize_mx(out=hid_codes[:].bitcast(E5M2), scales=hid_sc[:], in_=hid_bf[:].rearrange("p j t -> p (j t)"))
             for nt in range(N_TILES):
-                second_ps = ps.tile([P, HALF], F32, name=f"second_ps_{nt}_{h}")
                 nc.tensor.matmul_mx(
-                    out=second_ps[:],
+                    out=second_ps[(nt, h)],
                     lhsT=wb_sb[:, P * nt : P * (nt + 1)].bitcast(E4M3),
                     lhsT_scale=wb_sc[:, 0, P * nt : P * (nt + 1)],
                     rhs=hid_codes[:].bitcast(E5M2),
@@ -211,19 +234,17 @@ def tile_list_entryproducts_rival_scattered_kernel(
                     start=True,
                     stop=True,
                 )
-                if nt == 0 and h == 1:
-                    nc.vector.tensor_copy(result[nt][h][:], second_ps[:])
-                else:
-                    nc.scalar.copy(result[nt][h][:], second_ps[:])
-
-        for h in range(HALVES):
-            places = list_out[:, 8 * h : 8 * (h + 1)]
-            nc.vector.tensor_copy(pages[0][:].indirect(places), result[0][h][:])
-            nc.scalar.activation(pages[1][:].indirect(places), result[1][h][:], COPY)
+        nc.vector.tensor_copy(lead[:], lead_ps[:])
+        nc.scalar.copy(rest[:], rest_ps[:].rearrange("p s j -> p (s j)"))
+        nc.vector.tensor_copy(pages[0][:].indirect(list_out[:, : HALF // 16]), lead[:])
+        nc.vector.tensor_copy(pages[0][:].indirect(list_out[:, HALF // 16 :]), rest[:, :HALF])
+        nc.scalar.activation(pages[1][:].indirect(list_out[:]), rest[:, HALF:], COPY)
 
         for nt in range(N_TILES):
-            for c0 in range(0, C, STORE_COLS):
-                cols = slice(c0, c0 + STORE_COLS)
-                y = sb.tile([P, STORE_COLS], F32, name=f"y_{nt}_{c0}")
+            c0 = 0
+            for width in STORE_WIDTHS[nt]:
+                cols = slice(c0, c0 + width)
+                y = sb.tile([P, width], F32, name=f"y_{nt}_{c0}")
+                c0 = c0 + width
                 nc.vector.scalar_tensor_tensor(y[:], old_sb[:, nt, cols], 0.5, pages[nt][:, cols], ALU.mult, ALU.add)
                 nc.sync.dma_start(out=out[P * nt : P * (nt + 1), cols], in_=y[:])

@@ -24,7 +24,7 @@ PASSES = K // K_PASS
 HALF = 128
 HALVES = J // HALF
 N_TILES = N // P
-STORE_WIDTHS = ((256, 256, 512), (512, 256, 256))
+STORE_WIDTHS = ((256, 384, 384), (512, 512))
 
 
 def load_scale_rows(queue, plane, rows):
@@ -89,12 +89,14 @@ def tile_list_entryproducts_rival_scattered_kernel(
                 in_=rows[:, 4 * q : 4 * q + 4, :].rearrange("z r c -> r z c").bitcast(I32),
             )
 
+        nc.vector.memset(wb_sc[:].bitcast(I32), 0)
         nc.vector.memset(w_sc_raw[:].bitcast(I32), 0)
         nc.vector.memset(ws_sc_raw[:].bitcast(I32), 0)
         nc.vector.memset(sx_sc[:].bitcast(I32), 0)
-        nc.vector.memset(wb_sc[:].bitcast(I32), 0)
         for nt in range(N_TILES):
             nc.vector.memset(pages[nt][:], 0.0)
+        warm = sb.tile([P, 1], F32, name="warm")
+        nc.scalar.activation(warm[:], wb_sc[:, 0, 0:4].bitcast(F32), COPY)
 
         load_xb(0)
         nc.sync.dma_start(list_b[:], offs2)
@@ -108,18 +110,21 @@ def tile_list_entryproducts_rival_scattered_kernel(
         load_xb(1)
         load_scale_quadrant(w_sc_raw, w_scales, 3)
         load_words(ws_raw[:], ws_words.rearrange("z p c -> p z c"))
-        load_scale_quadrant(ws_sc_raw, ws_scales, 0)
         load_xa(0, 2)
-        for q in range(1, 4):
+        for q in (0, 1):
             load_scale_quadrant(ws_sc_raw, ws_scales, q)
         load_xa(0, 3)
+        for q in (2, 3):
+            load_scale_quadrant(ws_sc_raw, ws_scales, q)
         load_words(sx_sb[:], sx_words[0])
-        load_scale_quadrant(sx_sc, sx_scales, 0)
         load_xa(1, 0)
-        for q in range(1, 4):
+        for q in (0, 1):
             load_scale_quadrant(sx_sc, sx_scales, q)
-        for t in range(1, PACK):
-            load_xa(1, t)
+        load_xa(1, 1)
+        load_scale_quadrant(sx_sc, sx_scales, 2)
+        load_xa(1, 2)
+        load_scale_quadrant(sx_sc, sx_scales, 3)
+        load_xa(1, 3)
         load_words(wb_sb[:], wb_words[0].rearrange("p n t -> p (n t)"))
         load_scale_rows(nc.sync, wb_sc, wb_scales)
         nc.sync.dma_start(list_out[:], offs3)
@@ -139,7 +144,6 @@ def tile_list_entryproducts_rival_scattered_kernel(
         picked_b = [sb.tile([P, PACK, J], F32, name=f"picked_b_{z}") for z in range(PASSES)]
         factor = [sb.tile([P, PACK, J], F32, name=f"factor_{z}") for z in range(PASSES)]
         u = [sb.tile([P, PACK, J], F32, name=f"u_{z}") for z in range(PASSES)]
-        rival = [sb.tile([P, HALF, PACK], F32, name=f"rival_{h}") for h in range(HALVES)]
 
         def pick_b(z):
             for t in range(PACK):
@@ -178,8 +182,19 @@ def tile_list_entryproducts_rival_scattered_kernel(
         deal(ws_sc[:], ws_sc_raw[:])
         pick_a(1, 0, 0, J)
         pick_a(1, 1, 0, J)
+        first_ps = [ps.tile([P, PACK, HALF], F32, name=f"first_ps_{h}") for h in range(HALVES)]
+        nc.vector.quantize_mx(out=u0_codes[:].bitcast(E4M3), scales=u0_sc[:], in_=u0_bf[:].rearrange("p j t -> p (j t)"))
         for h in range(HALVES):
-            rival_ps = ps.tile([P, PACK, HALF], F32, name=f"rival_ps_{h}", tag=f"hidden_{h}")
+            cols = slice(HALF * h, HALF * (h + 1))
+            first_product(0, h, u0_codes[:, cols], u0_sc[:, cols])
+        pick_a(1, 2, 0, J)
+        pick_a(1, 3, 0, HALF)
+        picked_a = sb.tile([P, HALF], F32, name="picked_a", tag="picked_a_then_rival")
+        nc.scalar.activation(picked_a[:], xa_sb[1][3][:].indirect(list_a[:, HALF // 16 :]), COPY)
+        nc.vector.tensor_tensor(u[1][:, 3, HALF:], picked_a[:], factor[1][:, 3, HALF:], ALU.mult)
+        rival = sb.tile([P, HALVES, HALF, PACK], F32, name="rival", tag="picked_a_then_rival")
+        for h in range(HALVES):
+            rival_ps = ps.tile([P, PACK, HALF], F32, name=f"rival_ps_{h}")
             for t in range(PACK):
                 nc.tensor.matmul_mx(
                     out=rival_ps[:, t, :],
@@ -189,18 +204,8 @@ def tile_list_entryproducts_rival_scattered_kernel(
                     stop=True,
                     **stationary(ws_dealt, ws_sc, 0, t),
                 )
-            nc.scalar.copy(rival[h][:], rival_ps[:].rearrange("p t j -> p j t"))
+            nc.scalar.copy(rival[:, h], rival_ps[:].rearrange("p t j -> p j t"))
 
-        first_ps = [ps.tile([P, PACK, HALF], F32, name=f"first_ps_{h}", tag=f"hidden_{h}") for h in range(HALVES)]
-        nc.vector.quantize_mx(out=u0_codes[:].bitcast(E4M3), scales=u0_sc[:], in_=u0_bf[:].rearrange("p j t -> p (j t)"))
-        for h in range(HALVES):
-            cols = slice(HALF * h, HALF * (h + 1))
-            first_product(0, h, u0_codes[:, cols], u0_sc[:, cols])
-        pick_a(1, 2, 0, J)
-        pick_a(1, 3, 0, HALF)
-        picked_a = sb.tile([P, HALF], F32, name="picked_a")
-        nc.scalar.activation(picked_a[:], xa_sb[1][3][:].indirect(list_a[:, HALF // 16 :]), COPY)
-        nc.vector.tensor_tensor(u[1][:, 3, HALF:], picked_a[:], factor[1][:, 3, HALF:], ALU.mult)
         u1_bf = [sb.tile([P, HALF, PACK], BF16, name=f"u1_bf_{h}", align_bytes=64) for h in range(HALVES)]
         u1_codes = [sb.tile([P, HALF], U32, name=f"u1_codes_{h}", align_bytes=64) for h in range(HALVES)]
         u1_sc = [sb.tile([P, HALF], U8, name=f"u1_sc_{h}", align_bytes=64) for h in range(HALVES)]
@@ -222,7 +227,7 @@ def tile_list_entryproducts_rival_scattered_kernel(
             hid_bf = sb.tile([P, HALF, PACK], BF16, name=f"hid_bf_{h}", align_bytes=64)
             hid_codes = sb.tile([P, HALF], U32, name=f"hid_codes_{h}", align_bytes=64)
             hid_sc = sb.tile([P, HALF], U8, name=f"hid_sc_{h}", align_bytes=64)
-            nc.vector.tensor_tensor(hid_bf[:], first_ps[h][:].rearrange("p t j -> p j t"), rival[h][:], ALU.max)
+            nc.vector.tensor_tensor(hid_bf[:], first_ps[h][:].rearrange("p t j -> p j t"), rival[:, h], ALU.max)
             nc.vector.quantize_mx(out=hid_codes[:].bitcast(E5M2), scales=hid_sc[:], in_=hid_bf[:].rearrange("p j t -> p (j t)"))
             for nt in range(N_TILES):
                 nc.tensor.matmul_mx(

from contextlib import ExitStack

import concourse.mybir as mybir

K, T, J, S, R, L, N, C = 1024, 1024, 256, 512, 512, 512, 256, 1024
FLOPS = 2 * (K * R * J + L * R * J + R * N * J)

F32 = mybir.dt.float32
BF16 = mybir.dt.bfloat16
I32 = mybir.dt.int32
U32 = mybir.dt.uint32
U16 = mybir.dt.uint16
U8 = mybir.dt.uint8
E4M3 = mybir.dt.float8_e4m3fn_x4
E5M2 = mybir.dt.float8_e5m2_x4
E2M1 = mybir.dt.float4_e2m1fn_x4
ALU = mybir.AluOpType
COPY = mybir.ActivationFunctionType.Copy

P = 128
PACK = 4
K_PASS = P * PACK
PASSES = K // K_PASS
HALF = 128
HALVES = J // HALF
N_TILES = N // P
STORE_WIDTHS = ((256, 384, 384), (512, 512))


def load_scale_rows(queue, plane, rows):
    for q in range(4):
        queue.dma_start(
            out=plane[32 * q : 32 * q + 4].bitcast(I32),
            in_=rows[:, 4 * q : 4 * q + 4, :].rearrange("z r c -> r z c").bitcast(I32),
        )


def interleave(copy, dst, src):
    copy(
        dst.rearrange("p (c i) t -> p c t i", i=4),
        src.rearrange("p t (c i) -> p c t i", i=4),
    )


def tile_list_entryproducts_rival_scattered_kernel(
    tc, xa, xb, fk, w_words, w_scales, sx_words, sx_scales, ws_words, ws_scales, wb_words, wb_scales, old, offs, offs2, offs3, out
):
    nc = tc.nc
    with ExitStack() as ctx:
        sb = ctx.enter_context(tc.tile_pool(name="sb", bufs=1))
        ps = ctx.enter_context(tc.psum_pool(name="ps", bufs=1))

        list_a = sb.tile([P, J // 16], U16, name="list_a")
        list_b = sb.tile([P, J // 16], U16, name="list_b")
        list_out = sb.tile([P, J // 16], U16, name="list_out")
        fk_sb = sb.tile([P, PASSES, PACK], F32, name="fk_sb")
        xa_sb = [[sb.tile([P, T], F32, name=f"xa_{z}_{t}") for t in range(PACK)] for z in range(PASSES)]
        xb_sb = [sb.tile([P, PACK, S], F32, name=f"xb_{z}") for z in range(PASSES)]
        old_sb = sb.tile([P, N_TILES, C], F32, name="old_sb")

        w_raw = sb.tile([P, PASSES, 2 * R], U8, name="w_raw", align_bytes=64)
        ws_raw = sb.tile([P, 1, 2 * R], U8, name="ws_raw", align_bytes=64)
        w_dealt = sb.tile([P, PASSES, 2 * R], U8, name="w_dealt", align_bytes=64)
        ws_dealt = sb.tile([P, 1, 2 * R], U8, name="ws_dealt", align_bytes=64)
        w_sc_raw = sb.tile([P, PASSES, R], U8, name="w_sc_raw", align_bytes=64)
        ws_sc_raw = sb.tile([P, 1, R], U8, name="ws_sc_raw", align_bytes=64)
        w_sc = sb.tile([P, PASSES, R], U8, name="w_sc", align_bytes=64)
        ws_sc = sb.tile([P, 1, R], U8, name="ws_sc", align_bytes=64)
        sx_sb = sb.tile([P, 2 * J], U8, name="sx_sb", align_bytes=64)
        sx_sc = sb.tile([P, 1, J], U8, name="sx_sc", align_bytes=64)
        wb_sb = sb.tile([P, N], U32, name="wb_sb", align_bytes=64)
        wb_sc = sb.tile([P, 1, N], U8, name="wb_sc", align_bytes=64)
        pages = [sb.tile([P, C], F32, name=f"page_{nt}") for nt in range(N_TILES)]

        def load_xa(z, t):
            rows = xa[K_PASS * z : K_PASS * (z + 1), :].rearrange("(p t) c -> p t c", t=PACK)
            nc.sync.dma_start(out=xa_sb[z][t][:], in_=rows[:, t, :])

        def load_xb(z):
            rows = xb[K_PASS * z : K_PASS * (z + 1), :].rearrange("(p t) c -> p t c", t=PACK)
            nc.sync.dma_start(out=xb_sb[z][:], in_=rows)

        def load_words(dst, src):
            nc.sync.dma_start(out=dst.bitcast(I32), in_=src.bitcast(I32))

        def load_scale_quadrant(plane, rows, q):
            nc.sync.dma_start(
                out=plane[32 * q : 32 * q + 4].bitcast(I32),
                in_=rows[:, 4 * q : 4 * q + 4, :].rearrange("z r c -> r z c").bitcast(I32),
            )

        nc.vector.memset(wb_sc[:].bitcast(I32), 0)
        nc.vector.memset(w_sc_raw[:].bitcast(I32), 0)
        nc.vector.memset(ws_sc_raw[:].bitcast(I32), 0)
        nc.vector.memset(sx_sc[:].bitcast(I32), 0)
        for nt in range(N_TILES):
            nc.vector.memset(pages[nt][:], 0.0)
        warm = sb.tile([P, 1], F32, name="warm")
        nc.scalar.activation(warm[:], wb_sc[:, 0, 0:4].bitcast(F32), COPY)

        load_xb(0)
        nc.sync.dma_start(list_b[:], offs2)
        nc.sync.dma_start(out=fk_sb[:], in_=fk.rearrange("(z p t) o -> p z (t o)", p=P, t=PACK))
        load_xa(0, 0)
        nc.sync.dma_start(list_a[:], offs)
        load_words(w_raw[:], w_words.rearrange("z p c -> p z c"))
        load_xa(0, 1)
        for q in range(3):
            load_scale_quadrant(w_sc_raw, w_scales, q)
        load_xb(1)
        load_scale_quadrant(w_sc_raw, w_scales, 3)
        load_words(ws_raw[:], ws_words.rearrange("z p c -> p z c"))
        load_xa(0, 2)
        for q in (0, 1):
            load_scale_quadrant(ws_sc_raw, ws_scales, q)
        load_xa(0, 3)
        for q in (2, 3):
            load_scale_quadrant(ws_sc_raw, ws_scales, q)
        load_words(sx_sb[:], sx_words[0])
        load_xa(1, 0)
        for q in (0, 1):
            load_scale_quadrant(sx_sc, sx_scales, q)
        load_xa(1, 1)
        load_scale_quadrant(sx_sc, sx_scales, 2)
        load_xa(1, 2)
        load_scale_quadrant(sx_sc, sx_scales, 3)
        load_xa(1, 3)
        load_words(wb_sb[:], wb_words[0].rearrange("p n t -> p (n t)"))
        load_scale_rows(nc.sync, wb_sc, wb_scales)
        nc.sync.dma_start(list_out[:], offs3)
        nc.sync.dma_start(out=old_sb[:], in_=old.rearrange("(nt p) c -> p nt c", p=P))

        def deal(dst, src):
            nc.vector.tensor_copy(
                dst.rearrange("p z (t m) -> p z t m", t=PACK), src.rearrange("p z (m t) -> p z t m", t=PACK)
            )

        def stationary(dealt, scales, z, t):
            return dict(
                lhsT=dealt[:, z, 2 * P * t : 2 * P * (t + 1)].bitcast(E2M1),
                lhsT_scale=scales[:, z, P * t : P * (t + 1)],
            )

        picked_b = [sb.tile([P, PACK, J], F32, name=f"picked_b_{z}") for z in range(PASSES)]
        factor = [sb.tile([P, PACK, J], F32, name=f"factor_{z}") for z in range(PASSES)]
        u = [sb.tile([P, PACK, J], F32, name=f"u_{z}") for z in range(PASSES)]

        def pick_b(z):
            for t in range(PACK):
                nc.scalar.activation(picked_b[z][:, t, :], xb_sb[z][:, t, :].indirect(list_b[:]), COPY)
                nc.scalar.activation(factor[z][:, t, :], picked_b[z][:, t, :], COPY, scale=fk_sb[:, z, t : t + 1])

        def pick_a(z, t, first, count):
            cols = slice(first, first + count)
            entries = list_a[:, first // 16 : (first + count) // 16]
            nc.vector.tensor_tensor(u[z][:, t, cols], xa_sb[z][t][:].indirect(entries), factor[z][:, t, cols], ALU.mult)

        def first_product(z, h, codes, scales):
            for t in range(PACK):
                nc.tensor.matmul_mx(
                    out=first_ps[h][:, t, :],
                    rhs=codes.bitcast(E4M3),
                    rhs_scale=scales,
                    start=(z == 0 and t == 0),
                    stop=(z == PASSES - 1 and t == PACK - 1),
                    **stationary(w_dealt, w_sc, z, t),
                )

        pick_b(0)
        pick_a(0, 0, 0, J)
        deal(w_dealt[:].bitcast(U16), w_raw[:].bitcast(U16))
        pick_a(0, 1, 0, J)
        pick_b(1)
        deal(w_sc[:], w_sc_raw[:])
        deal(ws_dealt[:].bitcast(U16), ws_raw[:].bitcast(U16))
        pick_a(0, 2, 0, J)
        pick_a(0, 3, 0, J)
        u0_bf = sb.tile([P, J, PACK], BF16, name="u0_bf", align_bytes=64)
        u0_codes = sb.tile([P, J], U32, name="u0_codes", align_bytes=64)
        u0_sc = sb.tile([P, J], U8, name="u0_sc", align_bytes=64)
        interleave(nc.scalar.copy, u0_bf[:], u[0][:])
        deal(ws_sc[:], ws_sc_raw[:])
        pick_a(1, 0, 0, J)
        pick_a(1, 1, 0, J)
        first_ps = [ps.tile([P, PACK, HALF], F32, name=f"first_ps_{h}") for h in range(HALVES)]
        nc.vector.quantize_mx(out=u0_codes[:].bitcast(E4M3), scales=u0_sc[:], in_=u0_bf[:].rearrange("p j t -> p (j t)"))
        for h in range(HALVES):
            cols = slice(HALF * h, HALF * (h + 1))
            first_product(0, h, u0_codes[:, cols], u0_sc[:, cols])
        pick_a(1, 2, 0, J)
        pick_a(1, 3, 0, HALF)
        picked_a = sb.tile([P, HALF], F32, name="picked_a", tag="picked_a_then_rival")
        nc.scalar.activation(picked_a[:], xa_sb[1][3][:].indirect(list_a[:, HALF // 16 :]), COPY)
        nc.vector.tensor_tensor(u[1][:, 3, HALF:], picked_a[:], factor[1][:, 3, HALF:], ALU.mult)
        rival = sb.tile([P, HALVES, HALF, PACK], F32, name="rival", tag="picked_a_then_rival")
        for h in range(HALVES):
            rival_ps = ps.tile([P, PACK, HALF], F32, name=f"rival_ps_{h}")
            for t in range(PACK):
                nc.tensor.matmul_mx(
                    out=rival_ps[:, t, :],
                    rhs=sx_sb[:, 2 * HALF * h : 2 * HALF * (h + 1)].bitcast(E2M1),
                    rhs_scale=sx_sc[:, 0, HALF * h : HALF * (h + 1)],
                    start=True,
                    stop=True,
                    **stationary(ws_dealt, ws_sc, 0, t),
                )
            nc.scalar.copy(rival[:, h], rival_ps[:].rearrange("p t j -> p j t"))

        u1_bf = [sb.tile([P, HALF, PACK], BF16, name=f"u1_bf_{h}", align_bytes=64) for h in range(HALVES)]
        u1_codes = [sb.tile([P, HALF], U32, name=f"u1_codes_{h}", align_bytes=64) for h in range(HALVES)]
        u1_sc = [sb.tile([P, HALF], U8, name=f"u1_sc_{h}", align_bytes=64) for h in range(HALVES)]
        weavers = [nc.vector.tensor_copy, nc.vector.tensor_copy]
        for h in range(HALVES):
            interleave(weavers[h], u1_bf[h][:], u[1][:, :, HALF * h : HALF * (h + 1)])
        for h in range(HALVES):
            nc.vector.quantize_mx(
                out=u1_codes[h][:].bitcast(E4M3), scales=u1_sc[h][:], in_=u1_bf[h][:].rearrange("p j t -> p (j t)")
            )
            first_product(1, h, u1_codes[h][:], u1_sc[h][:])

        lead_ps = ps.tile([P, HALF], F32, name="lead_ps")
        rest_ps = ps.tile([P, 3, HALF], F32, name="rest_ps")
        second_ps = {(0, 0): lead_ps[:], (0, 1): rest_ps[:, 0, :], (1, 0): rest_ps[:, 1, :], (1, 1): rest_ps[:, 2, :]}
        lead = sb.tile([P, HALF], F32, name="lead")
        rest = sb.tile([P, 3 * HALF], F32, name="rest")
        for h in range(HALVES):
            hid_bf = sb.tile([P, HALF, PACK], BF16, name=f"hid_bf_{h}", align_bytes=64)
            hid_codes = sb.tile([P, HALF], U32, name=f"hid_codes_{h}", align_bytes=64)
            hid_sc = sb.tile([P, HALF], U8, name=f"hid_sc_{h}", align_bytes=64)
            nc.vector.tensor_tensor(hid_bf[:], first_ps[h][:].rearrange("p t j -> p j t"), rival[:, h], ALU.max)
            nc.vector.quantize_mx(out=hid_codes[:].bitcast(E5M2), scales=hid_sc[:], in_=hid_bf[:].rearrange("p j t -> p (j t)"))
            for nt in range(N_TILES):
                nc.tensor.matmul_mx(
                    out=second_ps[(nt, h)],
                    lhsT=wb_sb[:, P * nt : P * (nt + 1)].bitcast(E4M3),
                    lhsT_scale=wb_sc[:, 0, P * nt : P * (nt + 1)],
                    rhs=hid_codes[:].bitcast(E5M2),
                    rhs_scale=hid_sc[:],
                    start=True,
                    stop=True,
                )
        nc.vector.tensor_copy(lead[:], lead_ps[:])
        nc.scalar.copy(rest[:], rest_ps[:].rearrange("p s j -> p (s j)"))
        nc.vector.tensor_copy(pages[0][:].indirect(list_out[:, : HALF // 16]), lead[:])
        nc.vector.tensor_copy(pages[0][:].indirect(list_out[:, HALF // 16 :]), rest[:, :HALF])
        nc.scalar.activation(pages[1][:].indirect(list_out[:]), rest[:, HALF:], COPY)

        for nt in range(N_TILES):
            c0 = 0
            for width in STORE_WIDTHS[nt]:
                cols = slice(c0, c0 + width)
                y = sb.tile([P, width], F32, name=f"y_{nt}_{c0}")
                c0 = c0 + width
                nc.vector.scalar_tensor_tensor(y[:], old_sb[:, nt, cols], 0.5, pages[nt][:, cols], ALU.mult, ALU.add)
                nc.sync.dma_start(out=out[P * nt : P * (nt + 1), cols], in_=y[:])
